import numpy as np, ml_dtypes
CORES = [3,7,11,15,131,135,139,143]
N = 8
BF = ml_dtypes.bfloat16
def gentries(a):
    return np.ascontiguousarray(a.reshape(8, 16, -1).transpose(0, 2, 1)).reshape(8, -1)
def gtable(e):
    e = np.asarray(e); return np.ascontiguousarray(e.reshape(8, -1, 16).transpose(0, 2, 1)).reshape(128, -1).astype(np.int32)
L, T, B, RO = 2048, 2, 512, 3
W = L + T * B
def forest(rng, way):
    k = np.zeros((N, 8, RO, T, 2 * B), np.int64)
    for q in range(N):
        for g in range(8):
            for r in range(RO):
                free = np.ones(W, bool); m = int(way[q, g, r])
                for t in range(T):
                    pool = np.flatnonzero(free[:L + t * B])
                    if m == 0: p = rng.permutation(pool)[:2 * B]
                    elif m == 1: p = pool[:2 * B]
                    else: p = pool[len(pool) - 2 * B:]
                    if m > 0 and rng.random() < 0.5: p = rng.permutation(p)
                    free[p] = False; k[q, g, r, t] = p
    return k
def planned(rng, m, s):
    free = np.ones(W, bool); k = np.zeros((T, 2 * B), np.int64); order = rng.permutation(16); seq = None
    for t in range(T):
        pool = rng.permutation(np.flatnonzero(free[:L + t * B])); node = pool >= L; p = pool[:2 * B]
        if m == 0:
            late = node if t < 2 and t < T - 1 else ~node
            p = rng.permutation(pool[np.argsort(late, kind="stable")][:2 * B])
        elif m == 1 and t == 1:
            p = np.concatenate([pool[node], pool[~node][:B]])
        elif m == 2 and t == 1:
            p = np.concatenate([pool[~node][:B], pool[node]])
        elif m == 3:
            if t == 0:
                near = 128 * int(rng.integers(0, L // 128)) + rng.permutation(128); at = np.arange(2 * B)
                put = rng.permutation(np.flatnonzero(at % N == int(rng.integers(0, N))))[:128]
                rest = np.ones(2 * B, bool); rest[put] = False
                seq = np.zeros(2 * B, np.int64); seq[put] = near; seq[rest] = pool[~np.isin(pool, near)][:2 * B - 128]
            n = len(seq) // 2; slot = np.arange(n) if t == T - 1 else rng.permutation(B)[:n]
            p = np.zeros(2 * B, np.int64); rest = np.ones(2 * B, bool)
            rest[slot] = False; rest[B + slot] = False; p[slot] = seq[0::2]; p[B + slot] = seq[1::2]
            p[rest] = pool[~np.isin(pool, seq)][:2 * B - 2 * n]; seq = L + t * B + slot
        elif m == 4:
            two = np.isin(pool % 16, order[:2]); late = two if t < T - 1 else ~two
            p = rng.permutation(pool[np.argsort(late, kind="stable")][:2 * B])
        elif m == 5 and t == 0:
            p = rng.permutation(pool[np.argsort(order[pool % 16], kind="stable")][:2 * B])
        elif m == 6 and t == 0 and s is not None:
            p = p[np.argsort(s[p], kind="stable")]; i = rng.permutation(B); p = np.concatenate([p[:B][i], p[B:][i]])
        free[p] = False; k[t] = p
    return k
def parts(rng, way=None):
    x = rng.integers(-128, 128, (N, 8, 16, L)); k = forest(rng, np.zeros((N, 8, RO)) if way is None else way)
    a = rng.integers(-1, 2, (N, 8, 16, 16)); b = rng.integers(-1, 2, (N, 8, 16, 16)); w = rng.integers(-127, 128, (N, 8, 16))
    return x, k, a, b, w
def blocks(m):
    o = np.zeros((N, 8, 16, 8, 16), np.float32)
    for g in range(8): o[:, g, :, g, :] = m[:, g]
    return o.reshape(N, 128, 128).astype(BF)
def pack(x, k, a, b, w):
    return {"x": np.ascontiguousarray(x.reshape(N, 128, L)).astype(np.float32).astype(BF), "kids": np.stack([gtable(e.reshape(8, -1)) for e in k]),
            "ml": blocks(a), "mr": blocks(b), "w": w.reshape(N, 128, 1).astype(np.float32).astype(BF)}
def setup_inputs(rng):
    return pack(*parts(rng))
def setup_inputs_runs(rng):
    way = rng.choice(np.array([0, 1, 1, 2, 2]), (N, 8, RO)); i = rng.permutation(8); way[:, i[0]] = 1; way[:, i[1]] = 2
    return pack(*parts(rng, way))
def setup_inputs_ends(rng):
    x, k, a, b, w = parts(rng)
    x = rng.choice(np.array([-128, -127, -1, 0, 1, 126, 127]), (N, 8, 16, L))
    x[:, 0] = rng.integers(126, 128, (N, 16, L)); x[:, 1] = rng.integers(-128, -126, (N, 16, L)); a[:, :2] = 1; b[:, :2] = 1
    x[:, 2] = rng.choice(np.array([-128, 127]), (N, 1, L)); x[:, 2, 0] = rng.integers(-128, 128, (N, L)); a[:, 2] = 1; b[:, 2] = -1
    x[:, 3] = rng.integers(-2, 3, (N, 16, L))
    return pack(x, k, a, b, rng.choice(np.array([-127, 127]), (N, 8, 16)))
def setup_inputs_ties(rng):
    x, k, a, b, w = parts(rng)
    w[:, 0::4] = 0
    w[:, 1::4] = 0; w[:, 1::4, 0] = rng.integers(1, 128, (N, 2)); x[:, 1::4, 0] = rng.integers(-4, 5, (N, 2, L))
    for m in (a, b):
        m[:, 1::4, :, 0] = 0; m[:, 1::4, 0, 0] = 1
    v = rng.integers(-128, 128, (N, 2, 16, 1)); o = np.argsort(rng.random((N, 2, 16, L)), axis=2)
    x[:, 2::4] = np.take_along_axis(np.ascontiguousarray(np.broadcast_to(v, (N, 2, 16, L))), o, 2); w[:, 2::4] = rng.integers(1, 128, (N, 2, 1))
    x[:, 3::4, 2:] = 127; x[:, 3::4, 1] = rng.integers(-1, 2, (N, 2, L)); w[:, 3::4] = 127; w[:, 3::4, 0] = 0; w[:, 3::4, 1] = 1
    return pack(x, k, a, b, w)
def setup_inputs_crowd(rng):
    x, k, a, b, w = parts(rng); o = [int(g) for g in rng.permutation(8)]
    for i, v, c in ((2, 127, -1), (7, -127, 1)):
        x[:, o[i]] = np.where(rng.random((N, 1, L)) < 0.25, -128, rng.integers(-128, -99, (N, 16, L))); w[:, o[i]] = v; a[:, o[i]] = c; b[:, o[i]] = c
    w[:, o[3]] = 0
    for q in range(N):
        for i in range(8):
            s = np.add.reduce(w[q, o[i]][:, None] * x[q, o[i]], axis=0)
            for r in range(RO): k[q, o[i], r] = planned(rng, i if i < 7 else 1, s if r == 0 else None)
    return pack(x, k, a, b, w)
def setup_inputs_spread(rng):
    x, k, a, b, w = parts(rng)
    x = np.rint(127 * rng.uniform(-1, 1, (N, 8, 16, L)) * np.exp2(-rng.integers(0, 7, (N, 8, 1, L)).astype(np.float64))).astype(np.int64) * (rng.random((N, 8, 1, L)) > 0.0625)
    w = np.rint(127 * rng.uniform(-1, 1, (N, 8, 16)) * np.exp2(-rng.integers(0, 7, (N, 8, 16)).astype(np.float64))).astype(np.int64)
    s = rng.uniform(0.2, 1, (N, 8, 1, 1)); a = a * (rng.random(a.shape) < s); b = b * (rng.random(b.shape) < s)
    return pack(x, k, a, b, w)
def check_inputs(d):
    bad = []; own = np.kron(np.eye(8), np.ones((16, 16))) > 0
    for n, lo, hi in (("x", -128, 127), ("ml", -1, 1), ("mr", -1, 1), ("w", -127, 127)):
        v = np.asarray(d[n]).astype(np.float32)
        if not np.all((v == np.floor(v)) & (v >= lo) & (v <= hi)): bad.append("whole numbers of " + n)
        if n in ("ml", "mr") and not np.all(v[:, ~own] == 0): bad.append("zeros of " + n)
    k = np.stack([gentries(e) for e in d["kids"]]).astype(np.int64).reshape(N, 8, RO, T, 2 * B)
    for t in range(T):
        if np.min(k[:, :, :, t]) < 0 or np.max(k[:, :, :, t]) >= L + t * B: bad.append("range of kids")
    if not np.all(np.diff(np.sort(k.reshape(N, 8, RO, -1), axis=3), axis=3) > 0): bad.append("kids used twice")
    return bad
def reference(x, kids, ml, mr, w):
    leaf = x.astype(np.float64).reshape(N, 8, 16, L); ws = w.astype(np.float64).reshape(N, 8, 16, 1)
    cl, cr = [np.stack([m.astype(np.float64)[:, 16 * g:16 * g + 16, 16 * g:16 * g + 16] for g in range(8)], axis=1).transpose(0, 1, 3, 2) for m in (ml, mr)]
    kk = np.stack([gentries(e) for e in kids]).astype(np.int64).reshape(N, 8, RO, T, 2, B)
    for r in range(RO):
        h = np.zeros((N, 8, 16, W)); h[..., :L] = leaf
        size = np.ones((N, 8, W), np.int64); root = np.ones((N, 8, W), bool); order = []
        for t in range(T):
            a, b = kk[:, :, r, t, 0], kk[:, :, r, t, 1]; lo = L + t * B
            ha = np.take_along_axis(h, a[:, :, None, :], 3); hb = np.take_along_axis(h, b[:, :, None, :], 3)
            h[..., lo:lo + B] = np.clip(np.floor((np.matmul(cl, ha) + np.matmul(cr, hb)) * 0.25), -127, 127)
            size[..., lo:lo + B] = np.take_along_axis(size, a, 2) + np.take_along_axis(size, b, 2)
            swap = np.add.reduce(ws * ha, axis=2) < np.add.reduce(ws * hb, axis=2)
            np.put_along_axis(root, a, False, 2); np.put_along_axis(root, b, False, 2)
            order.append((np.where(swap, b, a), np.where(swap, a, b)))
        rs = np.where(root, size, 0); start = np.add.accumulate(rs, axis=2) - rs
        for t in range(T - 1, -1, -1):
            one, two = order[t]; s = start[..., L + t * B:L + t * B + B].copy()
            np.put_along_axis(start, one, s, 2); np.put_along_axis(start, two, s + np.take_along_axis(size, one, 2), 2)
        at = np.argsort(start[..., :L], axis=2)
        new = np.take_along_axis(leaf, at[:, :, None, :], 3).reshape(N, 8, 16, L // N, N)
        leaf = np.ascontiguousarray(new.transpose(4, 1, 2, 0, 3)).reshape(N, 8, 16, L)
    return {"y": leaf.reshape(N, 128, L).astype(np.float32).astype(BF)}

from concourse.mybir import AluOpType, ActivationFunctionType

N, RO, L, B = 8, 3, 2048, 512
H0, FS, QQ, PW = 2048, 2560, 3584, 5632
NB = PW // 16
NC = NB // 16
BW = 2560
MARK = (16.0, 128.0, 1024.0)
ACT_COLS = (48, 80, 96)
RELAY = ()
ORDER = "0517000c072f0a08090b011n062a0i271i0z2b0j0y280x251t0q2c3i131d29021r182d260o2g1e3j0g2h1o0p193k1a2e2i0k032j0l1p0n102k4w121f1s112l0m1q1v1j0s1u2m3l510r041k2n4x0u3m161h0v2o1w4y1b232p3n0t22142r2q0d1l1m1g1c524z3p2s0h0w1x50153q2t3o3r541y3v2u553s2v3t0e2w3u562x3w573x581z2y3y3z5940330f5a32202z4131307n21342453357o3742435b36443b5c385d3e39473a5e3c453f3d485f3g7t465g3h5i495h4f5j4c4a694l4b5k7v4d5l4i4g5m5u4e4o4j5n4m5o7p4p4h4k4r5p7q4s4q4t4n5t5s5r4u5q7u7r5v5w4v6b6a5y5z605x7s63616c6d6g6e7w6f7x6h6n626i7y6m6j6k7z6l656o6q806r666p6s646t6u676v6w6y8182686x6z8384707385717f7274867c76877579778978887a7i7d8a7g8l907l7e7j8b8c7k8d7b8e8f7h8g7m91928i938h8k94978j958m9896999e9d8n9a8o9h9b8p9c9i9g8u8q9j8r9k9f8s9l9m8t9n8w8v9p8x9q9o8y8z9r9ua0ac9s9v9t9xa3a9a69y9wa1a4a7aa9zaba5afa2a8ahaiajaeagalakad"
PICK = "111111101011110101111010100111111010011100110101011011111010101010"

S_, B_, F_, I_, U_ = "sbuf", "bfloat16", "float32", "int32", "uint16"
SCRATCH = {
    "K32": (S_, [128, 3, 128], I_), "H16": (S_, [128, 512], "float16"), "SZ": (S_, [128, 3, 32], B_),
    "V1": (S_, [128, 3, 32], F_), "LE": (S_, [128, 3, 32], F_), "U": (S_, [128, 3, 128], F_), "DL": (S_, [128, 3, 128], F_),
}
for _n in ("TA", "N1", "N0", "TT", "WW", "WN", "D2"):
    SCRATCH[_n] = (S_, [128, 3, 64], F_)
for _d, _l in ((B_, dict(pool0=PW, pool1=PW, pool2=PW, pool3=L, OUT=3 * L, AB=1024, GG=1024, Mv=FS, Z=1024, Bw=3 * BW, Bs=L, Bp=L,
                         ML=128, MR=128, ML4=128, MR4=128, Wc=8, Wp=32, Wn=32, ONE=160, TMP=128, TMQ=128, BO=128, BTI=128,
                         BTS=128, BTU=128, ZS=144, ZT=144, IP=160, XK=512, REP=128, C2=128, E8=512, JJ=48, VT=256, VW=NB + 8,
                         TW=64, EE=L, SB=256)),
               (F_, dict(Ma=FS, SRC=768, S8F=8, THR=128, PL=L, CF=12, END=3 * NB, CW=32, ST=64, T1=192, T2=192)),
               (I_, dict(THI=128, THJ=128, I2=NB, PB=NB, CI=8, CJ=8)),
               (U_, dict(K16=384, OB=32, LM=384, LF=384, LQ=192))):
    for _n, _w in _l.items():
        SCRATCH[_n] = (S_, [128, _w], _d)
for _b in range(8):
    SCRATCH["ps%d" % _b] = ("psum", [128, 512], F_)

SEMAPHORES = (["c_dve", "c_act", "c_pe", "c_pool", "d_kids", "d_x", "d_w", "d_ml", "d_mr", "d_z0", "d_z1", "d_z2",
               "d_y", "sent", "arr0", "arr1"] + ["last%d" % q for q in range(N)]
              + ["hop%d_%d" % (r, k) for r in range(RO) for k in RELAY])

CY = 0.83e-3 * 1.25
GA, SC, PEC = 1.56, 3.8, 0.55e-3
HOP, XFER, XLAT = 0.12, 0.75, 1.6


def send_order(T, topo, rank):
    core = T.cores[rank]
    kinds = [[], [], [], []]
    for k in range(N - 1, 0, -1):
        c = T.cores[rank ^ k]
        kinds[3 if c in topo.cores_of(core) else 2 if topo.mates(core, c) else 1 if topo.same_plane(core, c) else 0].append(rank ^ k)
    out = []
    while kinds[0] or kinds[1] or kinds[2]:
        out += [kinds[k].pop(0) for k in range(3) if kinds[k]]
    return out + kinds[3] + [rank]


def relays(T, topo, rank):
    core = T.cores[rank]
    order = send_order(T, topo, rank)
    free = [c for c in topo.cores_of(core) if c not in T.cores and topo.die(c) == topo.die(core)]
    reach = {c: sum(1 for d in T.cores if topo.may_write(c, d)) for c in free}
    load = {c: 0 for c in free}
    out = {}
    for k in RELAY:
        c = min([c for c in free if topo.may_write(c, T.cores[order[k]])], key=lambda c: (load[c], reach[c], c))
        load[c] += 1
        out[k] = c
    return out


def write(g, T, topo, src, dst, out, in_, sem):
    far = topo.engines(src, [c for c in T.cores if c not in topo.cores_of(src) and topo.may_write(src, c)][0])
    en = topo.engines(src, dst)
    en = [e for e in en if e not in far] or en
    rid, pid = topo.addr(dst, src)
    return g.remote_dma(out, in_, sem, T.sem.sent, pid, rid, sum(1 << e for e in en))


def landing(T, r, rank):
    return T["pool%d" % (r + 1)][:, 256 * rank:256 * rank + 256], T.sem["arr%d" % r if r < RO - 1 else "last%d" % rank]


def build(g, core, T, topo, rank):
    A = AluOpType
    F = ActivationFunctionType
    V, S = g.vector, g.scalar
    ops = []

    def al(b):
        return (b, 0, 1 << 20) if isinstance(b, str) else b

    def add(name, eng, fn, cost, r=(), w=(), lat=0.0, sem=None, ext=None, after=()):
        ops.append(dict(name=name, eng=eng if isinstance(eng, tuple) else (eng,), fn=fn, cost=cost, r=[al(x) for x in r],
                        w=[al(x) for x in w], lat=lat, sem=sem, ext=ext, after=list(after), id=len(ops)))
        return len(ops) - 1

    def dve(name, fn, n, r, w, f=1.0):
        return add(name, "dve", lambda e: fn(), max(64.0, n * f) * CY + 0.03, r, w)

    def ts(name, out, in0, s1, s2, o0, o1, n, r, w, f=1.0):
        if o1 is None:
            return dve(name, lambda: V.tensor_scalar(out, in0, s1, None, o0), n, r, w, f)
        return dve(name, lambda: V.tensor_scalar(out, in0, s1, s2, o0, o1), n, r, w, f)

    def tt(name, out, a, b, op, n, r, w, f=2.0):
        dve(name, lambda: V.tensor_tensor(out, a, b, op), n, r, w, f)

    def act(name, fn, n, r, w, extra=0.0):
        return add(name, "act", lambda e: fn(), max(64.0, n) * CY + 0.06 + extra, r, w)

    def mul(name, out, src, c, n, r, w):
        act(name, lambda: S.activation(out, src, F.Copy, scale=c), n, r, w)

    def pe(name, mms, r, w):
        return add(name, "pe", lambda e: [g.tensor.matmul(m[0], m[1], m[2], m[3], m[4]) for m in mms][-1],
                   sum(m[5] * PEC + 0.01 for m in mms) + 0.05, r, w)

    def iota(name, out, pat, base, ch, n, w, whole=False):
        if whole:
            return add(name, "pool", lambda e: g.iota(out, pat, base, ch), 0.17 + 2 * n * CY, [], [w])
        return add(name, "pool", lambda e: g.iota(out, pat, base, ch, allow_small_or_imprecise_dtypes=True), 0.17 + 2 * n * CY, [], [w])

    def copy(e, out, src):
        return V.tensor_copy(out, src) if e == "dve" else S.activation(out, src, F.Copy)

    def gather(name, calls, r, w, ext=None, after=()):
        return add(name, ("dve", "act"), lambda e: [copy(e, c[0], c[1]) for c in calls][-1],
                   sum(c[2] for c in calls) * GA * CY + 0.06 * len(calls), r, w, ext=ext, after=after)

    def dma(name, pairs, sem, lat, r, w, ext=None, after=()):
        return add(name, "sp", lambda e: [g.sync.dma_start(o, i).then_inc(T.sem[sem], 16) for o, i in pairs], 0.06 * len(pairs),
                   r, w, lat=lat, sem=(sem, 16 * len(pairs)), ext=ext, after=after)

    ps = [T["ps%d" % b] for b in range(8)]
    pn = ["ps%d" % b for b in range(8)]
    pools = [T["pool%d" % r] for r in range(4)]

    a = dma("ld_kids", [(T.K32[:], T.kids[:])], "d_kids", 2.0, [], ["K32"])
    a = dma("ld_x", [(T.pool0[:, 0:L], T.x[:])], "d_x", 4.0, [], [("pool0", 0, L)], after=[a])
    a = dma("ld_ml", [(T.ML[:], T.ml[:])], "d_ml", 2.4, [], ["ML"], after=[a])
    a = dma("ld_mr", [(T.MR[:], T.mr[:])], "d_mr", 2.4, [], ["MR"], after=[a])
    a = dma("ld_w", [(T.Wc[:, 0:1], T.w[:])], "d_w", 2.4, [], ["Wc"], after=[a])

    dve("z", lambda: V.memset(T.Z[:], 0.0), 1024, [], ["Z"], 0.5)
    dve("one", lambda: V.memset(T.ONE[:], 1.0), 160, [], ["ONE"], 0.5)
    dve("src0", lambda: V.memset(T.SRC[:, 0:256], MARK[0]), 256, [], [("SRC", 0, 256)])
    dve("mv", lambda: V.memset(T.Mv[:], 0.0), FS, [], ["Mv"], 0.5)
    act("ma0", lambda: S.activation(T.Ma[:, 0:1024], T.Z[:], F.Silu), 1024, ["Z"], [("Ma", 0, 1024)], 1.3)
    act("ma1", lambda: S.activation(T.Ma[:, 1024:1280], T.Z[:, 0:256], F.Copy), 256, ["Z"], [("Ma", 1024, 1280)])
    iota("ma2", T.Ma[:, 1280:L], [[0, 768]], 0, 0, 768, ("Ma", 1280, L))
    if max(ACT_COLS) > 64:
        iota("ma3", T.Ma[:, L:FS], [[0, B]], 0, 0, B, ("Ma", L, FS))
    for r in range(RO):
        a = dma("zb%d" % r, [(T.Bw[:, r * BW + k * 1024:r * BW + (k + 1) * 1024], T.Z[:]) for k in range(2)],
                "d_z%d" % r, 3.0, ["Z"], [("Bw", r * BW, r * BW + L)], after=[1, a])
    for r in (1, 2):
        iota("src%d" % r, T.SRC[:, 256 * r:256 * r + 256], [[0, 256]], int(MARK[r]), 0, 256, ("SRC", 256 * r, 256 * r + 256))

    def sel(name, out, lo, src, pat, op, base, ch, n):
        add(name, "pool", lambda e: g.affine_select(T[out][:, lo:lo + n], T[src][:, 0:n], pat, op, 0.0, base, ch),
            0.17 + 2 * n * CY, [src], [(out, lo, lo + n)])

    sel("bo1", "TMP", 0, "ONE", [[-16, 8], [0, 16]], A.is_ge, 0, 1, 128)
    sel("bo2", "BO", 0, "TMP", [[16, 8], [0, 16]], A.is_ge, 15, -1, 128)
    sel("rep1", "TMQ", 0, "ONE", [[0, 4], [-4, 32]], A.is_ge, 0, 1, 128)
    sel("rep2", "REP", 0, "TMQ", [[0, 4], [4, 32]], A.is_ge, 3, -1, 128)
    sel("ip", "IP", 0, "ONE", [[-1, 160]], A.is_equal, 32, 1, 160)
    for k in range(4):
        sel("xk%d" % k, "XK", 128 * k, "ONE", [[16, 8], [1, 4], [0, 4]], A.is_equal, 4 * k, -1, 128)
    sel("bti", "BTI", 0, "BO", [[1, 128]], A.is_ge, 0, -1, 128)
    sel("bts", "BTS", 0, "BO", [[1, 128]], A.is_gt, 0, -1, 128)
    sel("btu", "BTU", 0, "BO", [[-1, 128]], A.is_gt, 0, 1, 128)
    iota("thi", T.THI[:], [[0, 8], [-1, 4], [0, 4]], 128, 1, 128, "THI", True)
    ts("thj", T.THJ[:], T.THI[:], 3, None, A.bitwise_and, None, 128, ["THI"], ["THJ"])
    ts("thr", T.THR[:], T.THJ[:], -1.0e9, None, A.mult, None, 128, ["THJ"], ["THR"])
    iota("c2", T.C2[0:2, :], [[0, 128]], 12288, -12291, 128, "C2")
    dve("e8", lambda: V.memset(T.E8[0:32, :], 0.125), 512, [], ["E8"], 0.5)
    iota("i2", T.I2[:], [[1, NB]], 0, 1, NB, "I2", True)
    ts("pb", T.PB[:], T.I2[:], 1, None, A.arith_shift_right, None, NB, ["I2"], ["PB"])
    iota("jh", T.JJ[:, 0:NC], [[16, NC]], L, 0, NC, ("JJ", 0, 24))
    iota("jl", T.JJ[:, 24:24 + NC], [[0, NC]], 0, 1, NC, ("JJ", 24, 48))
    for h in range(4):
        iota("pl%d" % h, T.PL[:, B * h:B * h + B], [[1, 2], [128, 16], [8, 16]], 2 * h, 0, B, ("PL", B * h, B * h + B))
    iota("ci", T.CI[:, 0:2], [[-1, 2]], 1, 1, 2, "CI", True)
    ts("cj0", T.CJ[:, 0:1], T.CI[:, 0:1], 3, None, A.bitwise_and, None, 1, ["CI"], [("CJ", 0, 1)])
    ts("cj1", T.CJ[:, 4:5], T.CI[:, 1:2], 112, None, A.bitwise_and, None, 1, ["CI"], [("CJ", 4, 5)])
    ts("cf0", T.CF[:, 0:1], T.CJ[:, 0:1], 1.0, 2.0, A.add, A.max, 1, [("CJ", 0, 1)], [("CF", 0, 1)])
    ts("cf1", T.CF[:, 4:5], T.CJ[:, 4:5], 7.0, None, A.add, None, 1, [("CJ", 4, 5)], [("CF", 4, 5)])
    ts("cf2", T.CF[:, 8:9], T.CJ[:, 4:5], 16.0, 112.0, A.mult, A.add, 1, [("CJ", 4, 5)], [("CF", 8, 9)])
    mul("s8f", T.S8F[:], T.BO[:, 0:128:16], 1.0, 8, ["BO"], ["S8F"])
    mul("zs0", T.ZS[:], T.Z[:, 0:144], 1.0, 144, ["Z"], ["ZS"])
    dve("zs1", lambda: V.tensor_copy(T.ZS[:, 15:143:16], T.BO[:, 0:128:16]), 8, ["BO", "ZS"], ["ZS"])
    mul("zt", T.ZT[:], T.ZS[:], 2.0, 144, ["ZS"], ["ZT"])
    dve("vw", lambda: V.memset(T.VW[:, 0:1], 0.0), 1, [], [("VW", 0, 1)])
    dve("cw", lambda: V.memset(T.CW[:, 0:1], 0.0), 1, [], [("CW", 0, 1)])
    mul("ml4", T.ML4[:], T.ML[:], 0.25, 128, ["ML"], ["ML4"])
    mul("mr4", T.MR4[:], T.MR[:], 0.25, 128, ["MR"], ["MR4"])
    ts("wp", T.Wp[:], T.BO[:, 0:128:4], T.Wc[:, 0:1], None, A.mult, None, 32, ["BO", "Wc"], ["Wp"])
    ts("wn", T.Wn[:], T.BO[:, 0:128:4], T.Wc[:, 0:1], -1.0, A.mult, A.mult, 32, ["BO", "Wc"], ["Wn"])
    dve("k16a", lambda: V.tensor_copy(T.K16[:, 0:128], T.K32[:, 0, :]), 128, ["K32"], [("K16", 0, 128)])
    dve("k16b", lambda: V.tensor_copy(T.K16[:, 128:384], T.K32[:, 1:3, :]), 256, ["K32"], [("K16", 128, 384)])

    KL = T.K32[:, :, 64:128]
    ts("n1", T.N1[:], KL, float(L), 1.0, A.is_ge, A.add, 192, ["K32"], ["N1"])
    tt("sz", T.SZ[:], T.N1[:, :, 0:32], T.N1[:, :, 32:64], A.add, 96, ["N1"], ["SZ"])
    ts("ta", T.TA[:], KL, float(2 * H0 - FS), None, A.subtract, None, 192, ["K32"], ["TA"])
    tt("tt", T.TT[:], T.TA[:], T.N1[:], A.mult, 192, ["TA", "N1"], ["TT"])
    ts("n0", T.N0[:], KL, float(L), None, A.is_ge, None, 192, ["K32"], ["N0"])
    ts("u01", T.U[:, :, 0:64], T.TT[:], float(2 * H0 - FS), None, A.add, None, 192, ["TT"], ["Ua"])
    tt("dl0", T.DL[:, :, 0:32], T.TT[:, :, 32:64], T.TT[:, :, 0:32], A.subtract, 96, ["TT"], ["DLa"])
    mul("dl1", T.DL[:, :, 32:64], T.DL[:, :, 0:32], -1.0, 96, ["DLa"], ["DLb"])
    ts("ww", T.WW[:], T.DL[:, :, 0:64], -1.0, 1.0, A.mult, A.add, 192, ["DLa", "DLb"], ["WW"])
    tt("wn2", T.WN[:], T.WW[:], T.N0[:], A.mult, 192, ["WW", "N0"], ["WN"])
    tt("u2", T.U[:, :, 64:96], T.U[:, :, 32:64], T.WN[:, :, 0:32], A.add, 96, ["Ua", "WN"], ["Ub"])
    tt("v1", T.V1[:], T.U[:, :, 0:32], T.WN[:, :, 32:64], A.add, 96, ["Ua", "WN"], ["V1"])
    tt("dl2", T.DL[:, :, 64:96], T.V1[:], T.U[:, :, 64:96], A.subtract, 96, ["V1", "Ub"], ["DLc"])
    tt("u3", T.U[:, :, 96:128], T.U[:, :, 32:64], T.N0[:, :, 32:64], A.add, 96, ["Ua", "N0"], ["Uc"])
    tt("le", T.LE[:], T.U[:, :, 0:32], T.N0[:, :, 0:32], A.add, 96, ["Ua", "N0"], ["LE"])
    tt("dl3", T.DL[:, :, 96:128], T.LE[:], T.U[:, :, 96:128], A.subtract, 96, ["LE", "Uc"], ["DLd"])
    tt("d20", T.D2[:, :, 0:32], T.K32[:, :, 32:64], T.K32[:, :, 0:32], A.subtract, 96, ["K32"], ["D2a"])
    mul("d21", T.D2[:, :, 32:64], T.D2[:, :, 0:32], -1.0, 96, ["D2a"], ["D2b"])

    order = send_order(T, topo, rank)
    via = relays(T, topo, rank)
    arrive = [None] * 4
    for r in range(RO):
        s = str(r)
        P = pools[r]
        pr = "pool%d" % r
        k0 = 128 * r
        ac = ACT_COLS[r]
        kr = ("K16", k0, k0 + 128)
        sr = ("SRC", 256 * r, 256 * r + 256)
        src = T.SRC[:, 256 * r:256 * r + 256]
        wa = FS if ac > 64 else L
        for c in range(0, ac, 16):
            add("mka" + s, "act", lambda e, w=T.Ma[:, 0:wa].indirect(T.K16[:, k0 + c:k0 + c + 16]), src=src: S.activation(w, src, F.Silu),
                256 * SC * CY + 0.065, [kr, sr], [("Ma", 0, wa)])
        for c in range(ac, 128, 16):
            add("mkv" + s, "dve", lambda e, w=T.Mv[:].indirect(T.K16[:, k0 + c:k0 + c + 16]), src=src: V.tensor_copy(w, src),
                256 * SC * CY + 0.05, [kr, sr], ["Mv"])
        pe("mkZ" + s, [(ps[3][:, 0:192], T.Z[0:1, 0:128], T.Z[0:1, 0:192], True, False, 192)], ["Z"], [pn[3]])
        for name, win, rhs, c, nodes in (("Ma", T.Ma, T.S8F[:], 256, ac > 64), ("Mv", T.Mv, T.BO[:, 0:128:16], 64, True)):
            if name == "Mv" and ac == 128:
                continue
            mm = [(ps[3][0:64, 128 + k:192:8], win[:, H0 + k:FS:8], rhs, False, False, c) for k in range(8) if nodes]
            mm += [(ps[3][:, p:128:16], win[:, p:L:16], rhs, False, p == 15 and (name == "Mv" or ac == 128), c) for p in range(16)]
            st = 4 if name == "Ma" else 12
            for i in range(0, len(mm), st):
                pe("mk" + name + s, mm[i:i + st], [(name, 0, wa if name == "Ma" else FS), "BO", "S8F"], [pn[3]])
        act("vt" + s, lambda sc=-2.0 / MARK[r]: [S.activation(o, i, F.Relu, bias=16.0, scale=sc) for o, i in (
            (T.VT[0:64, 128:256:2], ps[3][0:64, 128:192]), (T.VT[0:64, 129:256:2], ps[3][0:64, 128:192]),
            (T.VT[:, 0:128], ps[3][:, 0:128]))][-1], 380, [pn[3]], ["VT"])
        mm = [(ps[4][:, 224 + k:NB:4], T.XK[:, 128 * k:128 * k + 128], T.SZ[:, r, :], True, True, 64) for k in range(4)]
        mm += [(ps[4][:, 128:224], T.VT[0:64, 128:256], T.IP[0:64, 0:96], True, True, 96),
               (ps[4][:, 0:128], T.VT[:, 0:128], T.IP[:, 32:160], True, True, 128)]
        pe("vW" + s, mm, ["XK", "SZ", "VT", "IP"], [pn[4]])
        ts("vw" + s, T.VW[:, 1:1 + NB], ps[4][:, 0:NB], T.CF[:, 0:1], None, A.is_ge, None, NB, [pn[4], ("CF", 0, 1)], [("VW", 1, 1 + NB)])
        pe("totW" + s, [(ps[5][:, NB:NB + NC], T.ZS[:, 15 - p:143 - p], T.VW[:, 1 + p:1 + NB:16], p == 0, p == 15, 64)
                        for p in range(16)], ["ZS", "VW"], [pn[5]])
        act("tw" + s, lambda: [S.activation(T.TW[:, o:o + NC], ps[5][:, NB:NB + NC], F.Copy, scale=c)
                               for o, c in ((0, 1.0), (32, -4096.0))][-1], 150, [pn[5]], ["TW"])
        pe("inc" + s, [(ps[6][:, 0:NB], T.BTI[:], T.VW[:, 1:1 + NB], True, False, NB),
                       (ps[6][:, 0:NB], T.BTU[:], T.VW[:, 0:NB], False, True, NB)], ["BTI", "BTU", "VW"], [pn[6]])
        I = T.IP[:, 32:160]
        pe("cs" + s, [(ps[5][:, 384:384 + NC], T.BO[:], T.TW[:, 0:NC], True, True, 64),
                      (ps[5][:, 416:416 + NC], T.BTS[:], T.TW[:, 0:NC], True, True, 64),
                      (ps[5][:, 448:448 + NC], I, T.JJ[:, 0:NC], True, False, 64),
                      (ps[5][:, 448:448 + NC], I, T.JJ[:, 24:24 + NC], False, False, 64),
                      (ps[5][:, 448:448 + NC], I, T.TW[:, 32:32 + NC], False, True, 64)],
           ["BO", "BTS", "IP", "JJ", "TW"], [pn[5]])
        dve("cw" + s, lambda: V.tensor_tensor_scan(T.CW[:, 1:1 + NC], T.ONE[:, 0:NC], ps[5][:, 384:384 + NC], 0.0, A.mult, A.add),
            NC, [pn[5], "ONE"], [("CW", 1, 32)])
        tt("st" + s, T.ST[:, 0:NC], T.CW[:, 0:NC], ps[5][:, 416:416 + NC], A.add, NC, [pn[5], "CW"], [("ST", 0, 32)])
        tt("sj" + s, T.ST[:, 32:32 + NC], T.ST[:, 0:NC], ps[5][:, 448:448 + NC], A.max, NC, [pn[5], ("ST", 0, 32)], [("ST", 32, 64)])
        dve("ob" + s, lambda: V.tensor_copy(T.OB[:, 0:NC], T.ST[:, 32:32 + NC]), NC, [("ST", 32, 64)], ["OB"])
        W = T.Bw[:, r * BW:r * BW + L]
        add("bsc" + s, "dve", lambda e, r=r: V.tensor_copy(T.Bw[:, r * BW:(r + 1) * BW].indirect(T.OB[:, 0:NC]), T.PB[:]),
            NB * SC * CY + 0.05, ["OB", "PB"], [("Bw", r * BW, (r + 1) * BW)])
        dve("bs" + s, lambda W=W: V.tensor_tensor_scan(T.Bs[:], W, W, 0.0, A.max, A.max), L, [("Bw", r * BW, r * BW + L)], ["Bs"], 0.5)
        for d in range(0, N, 2):
            add("bp" + s, ("dve", "act"), lambda e, d=d: [copy(e, T.Bp[:, 256 * k:256 * k + 256], T.Bs[:, k:L:8]) for k in (d, d + 1)][-1],
                256 * CY + 0.06, ["Bs"], [("Bp", 256 * d, 256 * d + B)])
        e0 = NB * r
        END = T.END[:, e0:e0 + NB]
        dve("end" + s, lambda END=END: V.tensor_tensor_scan(END, T.Z[:, 0:NB], ps[6][:, 0:NB], 0.0, A.add, A.add), NB,
            [pn[6], "Z"], [("END", e0, e0 + NB)])
        for i in (0, 8):
            pe("mW" + s, [(ps[6][:, 0:128], T.ZS[:, 15 - p:143 - p], T.Bp[:, p:L:16], p == 0, p == 15, 128) for p in range(i, i + 8)],
               ["Bp", "ZS"], [pn[6]])
        ts("lm" + s, T.LM[:, k0:k0 + 128], ps[6][:, 0:128], 0.125, T.CF[:, 4:5], A.mult, A.subtract, 128, [pn[6], ("CF", 4, 5)],
           [("LM", k0, k0 + 128)])
        for i in (0, 4, 8, 12):
            pe("fM" + s, [(ps[7][:, 0:128], T.ZT[:, 15 - p:143 - p], T.Bp[:, p:L:16], p == 0, False, 128) for p in range(i, i + 4)],
               ["Bp", "ZT"], [pn[7]])
        for h in range(4):
            add("ee%d" % h + s, "dve", lambda e, h=h, w=END.indirect(T.LM[:, k0 + 32 * h:k0 + 32 * h + 32]): V.tensor_tensor(
                T.EE[:, B * h:B * h + B], w, T.PL[:, B * h:B * h + B], A.is_le),
                B * GA * CY + 0.05, [("END", e0, e0 + NB), ("LM", k0, k0 + 128), ("PL", B * h, B * h + B)], [("EE", B * h, B * h + B)])
            if h % 2:
                lo = B * (h - 1)
                pe("fW%d" % h + s, [(ps[7][:, lo // 16:lo // 16 + 64], T.ZS[:, 15 - p:143 - p], T.EE[:, lo + p:lo + 1024:16],
                                     False, h == 3 and p == 15, 64) for p in range(16)], ["ZS", ("EE", lo, lo + 1024)], [pn[7]])
        ts("lf" + s, T.LF[:, k0:k0 + 128], ps[7][:, 0:128], T.CF[:, 8:9], None, A.subtract, None, 128, [pn[7], ("CF", 8, 9)],
           [("LF", k0, k0 + 128)])

        ext = None if r == 0 else ("arr%d" % (r - 1), 8 * (N - 1))
        aft = [] if r == 0 else [arrive[r]]
        pe("pre" + s, [(ps[0][:, 0:B], T.C2[0:2, :], T.E8[0:2, :], True, False, B)], ["C2", "E8"], [pn[0]])
        for h in range(2):
            gather("ab%d" % h + s, [(T.AB[:, B * h:B * h + B], P[:, 0:L].indirect(T.K16[:, k0 + 32 * h:k0 + 32 * h + 32]), B)],
                   [(pr, 0, L), kr], [("AB", B * h, B * h + B)], ext, aft)
        pe("sA" + s, [(ps[0][:, 0:B], T.ML4[:], T.AB[:, 0:B], False, False, B)], ["ML4", ("AB", 0, B)], [pn[0]])
        pe("sB" + s, [(ps[0][:, 0:B], T.MR4[:], T.AB[:, B:2 * B], False, True, B)], ["MR4", ("AB", B, 2 * B)], [pn[0]])
        ts("c1" + s, T.H16[:], ps[0][:, 0:B], 1409.0, 1663.0, A.max, A.min, B, [pn[0]], ["H16"])
        ts("c2" + s, P[:, H0:FS], T.H16[:], 1536.0, None, A.subtract, None, B, ["H16"], [(pr, H0, FS)], 0.5)

        def swap(tag, buf, name, n, o, tab, dtab, rd):
            mm = []
            for a in range(4):
                mm.append((ps[1][:, a:128:4], buf[:, a:B:4], T.Wp[:], True, False, 64))
                mm.append((ps[1][:, a:128:4], buf[:, B + a:2 * B:4], T.Wn[:], False, True, 64))
            so = 128 if o else 0
            pe("dT" + tag, mm, [name, "Wp", "Wn"], [pn[1]])
            tt("sb" + tag, T.SB[:, so:so + 128], ps[1][:, 0:128], T.THR[:], A.is_lt, 128, [pn[1], "THR"], [("SB", so, so + 128)], 1.0)
            pe("sW" + tag, [(ps[2][:, 0:n], T.SB[:, so:so + 128], T.REP[:, 0:n], True, True, max(n, 64))],
               [("SB", so, so + 128), "REP"], [pn[2]])
            tt("t1" + tag, T.T1[:, o:o + n], ps[2][:, 0:n], dtab, A.mult, n, [pn[2]] + rd, [("T1", o, o + n)], 1.0)
            tt("t2" + tag, T.T2[:, o:o + n], T.T1[:, o:o + n], tab, A.add, n, [("T1", o, o + n)] + rd, [("T2", o, o + n)])
            dve("lq" + tag, lambda: V.tensor_copy(T.LQ[:, o:o + n], T.T2[:, o:o + n]), n, [("T2", o, o + n)], [("LQ", o, o + n)])

        swap("0" + s, T.AB, "AB", 64, 0, T.K32[:, r, 0:64], T.D2[:, r, :], ["K32", "D2a", "D2b"])
        for h in range(2):
            gather("gg%d" % h + s, [(T.GG[:, B * h:B * h + B], P[:, 0:FS].indirect(T.K16[:, k0 + 64 + 32 * h:k0 + 96 + 32 * h]), B)],
                   [(pr, 0, FS), kr], [("GG", B * h, B * h + B)], ext, aft)
        for h in range(2):
            lo = FS + B * h
            gather("fs%d" % h + s, [(P[:, lo + o:lo + B:2], P[:, 0:L].indirect(T.LQ[:, 32 * o + 16 * h:32 * o + 16 * h + 16]), 256)
                                    for o in range(2)], [(pr, 0, L), ("LQ", 0, 64)], [(pr, lo, lo + B)], ext, aft)
        swap("1" + s, T.GG, "GG", 128, 64, T.U[:, r, :], T.DL[:, r, :], ["Ua", "Ub", "Uc", "DLa", "DLb", "DLc", "DLd"])
        for h in range(4):
            lo = QQ + 1024 * (h // 2)
            c0 = 64 + 16 * (h // 2)
            gather("qq%d" % h + s, [(P[:, lo + (0, 2, 1, 3)[k]:lo + 1024:4], P[:, 0:QQ].indirect(T.LQ[:, c0 + 32 * k:c0 + 32 * k + 16]), 256)
                                    for k in (2 * (h % 2), 2 * (h % 2) + 1)], [(pr, 0, QQ), ("LQ", 64, 192)], [(pr, lo, lo + 1024)],
                   ext, aft)
        xs = []
        prev = []
        for k, d in enumerate(order):
            lst = T.LF[:, k0 + 16 * d:k0 + 16 * d + 16]
            rd = [pr, ("LF", k0 + 16 * d, k0 + 16 * d + 16)]
            land, sem = landing(T, r, rank)
            if d == rank:
                gather("fin" + s, [(land, P[:].indirect(lst), 256)], rd, [("pool%d" % (r + 1), 256 * d, 256 * d + 256)], ext, aft)
                continue
            lo = L * r + 256 * d
            piece = T.OUT[:, lo:lo + 256]
            gather("fin" + s, [(piece, P[:].indirect(lst), 256)], rd, [("OUT", lo, lo + 256)], ext, aft)
            c = T.cores[d]
            if k in via:
                c, land, sem = via[k], piece, T.sem["hop%d_%d" % (r, k)]
            o = add("send" + s, "pool", lambda e, c=c, land=land, piece=piece, sem=sem: write(g, T, topo, core, c, land, piece, sem),
                    0.2, [("OUT", lo, lo + 256)], [], sem=("none", 0), after=prev)
            prev = [o]
            x = add("xfer", "near" if c in topo.cores_of(core) else "far", None, XFER, after=[o], lat=XLAT)
            if k in via:
                x = add("xfer", "via%d" % sorted(set(via.values())).index(c), None, XFER, after=[x], lat=XLAT)
            xs.append((x, d))
        arrive[r + 1] = add("arrive", "net", None, 0.001, after=[x[0] for x in xs])
        if r == RO - 1:
            dma("st", [(T.y[:, 256 * rank:256 * rank + 256], T.pool3[:, 256 * rank:256 * rank + 256])], "d_y", 2.0,
                [("pool3", 256 * rank, 256 * rank + 256)], [])
            for x, d in xs:
                dma("st", [(T.y[:, 256 * d:256 * d + 256], T.pool3[:, 256 * d:256 * d + 256])], "d_y", 2.0, [], [],
                    ext=("last%d" % d, 8), after=[x])
    return ops


def depend(ops):
    seen = {}
    for o in ops:
        dep = {a: None for a in o["after"]}
        acc = [(x, False) for x in o["r"]] + [(x, True) for x in o["w"]]
        for x, wr in acc:
            for (j, lo, hi, w2) in seen.get(x[0], []):
                if lo < x[2] and x[1] < hi:
                    if x[0][:2] == "ps":
                        dep[j] = dep.get(j) or "bank"
                    elif w2 or wr:
                        dep[j] = "raw"
        for x, wr in acc:
            seen.setdefault(x[0], []).append((o["id"], x[1], x[2], wr))
        o["dep"] = dep


DIGITS = "0123456789abcdefghijklmnopqrstuvwxyz"


def schedule(ops):
    ids = [DIGITS.index(ORDER[2 * k]) * 36 + DIGITS.index(ORDER[2 * k + 1]) for k in range(len(ops))]
    pick = iter(PICK)
    for i in ids:
        ops[i]["on"] = ops[i]["eng"][int(next(pick)) if len(ops[i]["eng"]) > 1 else 0]
    return [ops[i] for i in ids]


def emit(g, T, ops, seq):
    queues = {"dve": g.vector, "act": g.scalar, "pe": g.tensor, "pool": g, "sp": g.sync}
    pos, cnt, at = {}, {}, {}
    for k, o in enumerate(seq):
        at[o["id"]] = k
        if o["fn"] is not None and o["sem"] is None:
            cnt[o["on"]] = cnt.get(o["on"], 0) + 1
            pos[o["id"]] = cnt[o["on"]]
    know = {q: {} for q in queues}
    clock = {}
    waited = set()
    seq = [o for o in seq if o["fn"] is not None]
    for o in seq:
        q = o["on"]
        need = [] if o["ext"] is None else [(o["ext"][0], o["ext"][1], None)]
        for j, kind in o["dep"].items():
            p = ops[j]
            if kind is None or (p["on"] == q and p["sem"] is None and (q == "pe" or kind == "bank")):
                continue
            need.append((p["sem"][0], p["sem"][1], j) if p["sem"] else ("c_" + p["on"], pos[j], j))
        need.sort(key=lambda x: 1 if x[2] is None else -at[x[2]])
        o["waits"] = []
        for key, val, j in need:
            if know[q].get(key, 0) < val:
                o["waits"].append((key, val, j))
                know[q][key] = val
                if j is not None:
                    waited.add(j)
                    for k2, v2 in clock[j].items():
                        know[q][k2] = max(know[q].get(k2, 0), v2)
        clock[o["id"]] = dict(know[q])
    num, cnt = {}, {}
    for o in seq:
        if o["id"] in waited and o["id"] in pos:
            cnt[o["on"]] = cnt.get(o["on"], 0) + 1
            num[o["id"]] = cnt[o["on"]]
    for o in seq:
        for key, val, j in o["waits"]:
            queues[o["on"]].wait_ge(T.sem[key], num[j] if j in num else val)
        ins = o["fn"](o["on"])
        if o["id"] in num:
            ins.then_inc(T.sem["c_" + o["on"]], 1)
    g.sync.wait_ge(T.sem.d_y, 16 * N)
    g.wait_ge(T.sem.sent, 8 * (N - 1) * RO)


def hand_on(g, core, T, topo):
    n = 0
    for rank in range(N):
        mine = [k for k, c in sorted(relays(T, topo, rank).items()) if c == core]
        order = send_order(T, topo, rank)
        for r in range(RO):
            for k in mine:
                lo = L * r + 256 * order[k]
                land, sem = landing(T, r, rank)
                g.wait_ge(T.sem["hop%d_%d" % (r, k)], 8)
                write(g, T, topo, core, T.cores[order[k]], land, T.OUT[:, lo:lo + 256], sem)
                n += 8
    if n:
        g.wait_ge(T.sem.sent, n)


def rank_program(g, core, T, topo):
    rank = T.rank_of(core)
    if rank is None:
        if RELAY:
            hand_on(g, core, T, topo)
        return
    ops = build(g, core, T, topo, rank)
    depend(ops)
    emit(g, T, ops, schedule(ops))
